import numpy as np
import ml_dtypes


def mxq(x, axis, fmt="e4m3"):
    dtype, down = {"e4m3": (ml_dtypes.float8_e4m3fn, 7), "e5m2": (ml_dtypes.float8_e5m2, 14)}[fmt]
    v = np.moveaxis(np.asarray(x, np.float32).astype(ml_dtypes.bfloat16).astype(np.float64), axis, -1)
    blocks = v.reshape(v.shape[:-1] + (-1, 32))
    amax = np.abs(blocks).max(-1, keepdims=True)
    byte = np.maximum(np.where(amax > 0, np.frexp(amax)[1] - 1 + 127, 0) - down, 1)
    scale = np.exp2(byte - 127.0)
    codes = (blocks / scale).astype(np.float32).astype(dtype).astype(np.float64)
    return np.moveaxis((codes * scale).reshape(v.shape), -1, axis)


WIDE = False


def mx_kscale(k):
    if not WIDE:
        return np.ones(k)
    levels = np.array([30, -30])
    if k % 512:
        return np.exp2(np.random.permutation(np.resize(levels, k // 32))).repeat(32)
    a = np.empty((k // 512, 16))
    for p in range(k // 512):
        a[p, :8] = np.random.permutation(np.resize(levels, 8))
        for g in range(8):
            far = levels[np.abs(levels - a[p, g]) >= 10]
            a[p, g + 8] = far[np.random.randint(len(far))]
    return np.exp2(a.ravel()).repeat(32)


def f64(x):
    return np.asarray(x).astype(np.float64)


def striped(idx):
    return np.tile(np.asarray(idx).reshape(-1, 16).T, (8, 1)).astype(np.uint16)


def unstriped(offs):
    return offs[:16].T.reshape(-1).astype(np.int64)


E2M1 = np.array([0.0, 0.5, 1.0, 1.5, 2.0, 3.0, 4.0, 6.0, -0.0, -0.5, -1.0, -1.5, -2.0, -3.0, -4.0, -6.0])


def pack_weight(w, fmt):
    k, n = w.shape
    w = f64(np.asarray(w, np.float32).astype(ml_dtypes.bfloat16)).reshape(k // 32, 32, n)
    amax = np.abs(w).max(1)
    if fmt in ("e4m3", "e5m2"):
        byte = np.frexp(amax)[1] - 1 + 127 - (7 if fmt == "e4m3" else 14)
    else:
        mant, ex = np.frexp(amax / 6.0)
        byte = np.where(mant > 0.5, ex, ex - 1) + 127
    byte = np.clip(np.where(amax > 0, byte, 1), 1, 254)
    scaled = (w * np.exp2(127.0 - byte)[:, None, :]).reshape(k, n).astype(np.float32)
    by_word = np.ascontiguousarray(scaled.reshape(k // 512, 128, 4, n).transpose(0, 1, 3, 2))
    if fmt in ("e4m3", "e5m2"):
        words = by_word.astype(ml_dtypes.float8_e4m3fn if fmt == "e4m3" else ml_dtypes.float8_e5m2).view(np.uint8)
    else:
        c = by_word.astype(ml_dtypes.float4_e2m1fn).view(np.uint8) & 0xF
        words = (c[..., 0::2] | (c[..., 1::2] << 4)).reshape(k // 512, 128, 2 * n)
    return np.ascontiguousarray(words), np.ascontiguousarray(byte.astype(np.uint8).reshape(k // 512, 16, n))


def unpack_weight(words, scales, fmt):
    g, _, n = scales.shape
    words = np.ascontiguousarray(words).reshape(g, 128, n, -1)
    if fmt in ("e4m3", "e5m2"):
        vals = words.view(ml_dtypes.float8_e4m3fn if fmt == "e4m3" else ml_dtypes.float8_e5m2).astype(np.float64)
    else:
        nib = np.empty((g, 128, n, 4), np.uint8)
        nib[..., 0::2] = words & 0xF
        nib[..., 1::2] = words >> 4
        vals = E2M1[nib]
    vals = vals * np.repeat(np.exp2(scales.astype(np.float64) - 127.0), 8, axis=1)[..., None]
    return vals.transpose(0, 1, 3, 2).reshape(g * 512, n)


def bf(x):
    return np.asarray(x, np.float32).astype(ml_dtypes.bfloat16)


def planes(Y):
    r, m = Y.shape
    b = f64(bf(Y)).reshape(r // 32, 32, m)
    amax = np.abs(b).max(1)
    byte = np.clip(np.where(amax > 0, np.frexp(amax)[1] - 1 + 127 - 7, 1), 1, 254)
    codes = (b * np.exp2(127.0 - byte)[:, None, :]).reshape(r, m).astype(np.float32).astype(ml_dtypes.float8_e4m3fn).view(np.uint8)
    words = codes.reshape(r // 512, 128, 4, m).transpose(0, 1, 3, 2)
    return np.ascontiguousarray(words), np.ascontiguousarray(byte.astype(np.uint8).reshape(r // 512, 16, m))


K, T, J, R, N, Z = 512, 512, 256, 512, 512, 512


def setup_inputs():
    n = np.random.standard_normal
    idx = np.random.permutation(T)[:J]
    idx2 = np.random.permutation(Z)[:J]
    fk = mx_kscale(K)
    fr = mx_kscale(R)
    xtp = pack_weight(n((K, T)) / fk[:, None], "e2m1")
    wp = pack_weight(n((K, R)) * 1 / np.sqrt(K) * fk[:, None], "e5m2")
    wbp = pack_weight(n((R, N)) * 1 / np.sqrt(R) / fr[:, None], "e4m3")
    return {
        "xt_words": xtp[0],
        "xt_scales": xtp[1],
        "w_words": wp[0],
        "w_scales": wp[1],
        "us": (np.random.uniform(0.5, 1.5, (1, R)) * fr).astype(np.float32),
        "wb_words": wbp[0],
        "wb_scales": wbp[1],
        "tz": (n((N, Z)) * 0.6).astype(np.float32),
        "rw": (np.random.uniform(0.5, 2.0, (1, J))).astype(np.float32),
        "offs": striped(idx),
        "offs2": striped(idx2),
    }


def reference(xt_words, xt_scales, w_words, w_scales, us, wb_words, wb_scales, tz, rw, offs, offs2):
    idx = unstriped(offs)
    idx2 = unstriped(offs2)
    xtu = unpack_weight(xt_words, xt_scales, "e2m1")
    wu = unpack_weight(w_words, w_scales, "e5m2")
    wbu = unpack_weight(wb_words, wb_scales, "e4m3")
    xtidxg = xtu[:, idx]
    a = xtidxg.T @ wu
    m1 = np.max(a, axis=1, keepdims=True)
    hr = np.maximum(a, 0.0) / (m1 + 0.3) * f64(us)
    hid = hr.T
    hidq = mxq(hid, 0, "e5m2")
    p = wbu.T @ hidq
    y = np.maximum(p, f64(tz)[:, idx2]) * f64(rw)
    words, scales = planes(y)
    return y, words, scales

@@ -1,0 +1,169 @@
+from contextlib import ExitStack
+
+import concourse.mybir as mybir
+from concourse.masks import make_identity
+
+K, T, J, R, N, Z = 512, 512, 256, 512, 512, 512
+FLOPS = 2 * J * K * R + 2 * J * R * N
+
+F32 = mybir.dt.float32
+BF16 = mybir.dt.bfloat16
+I32 = mybir.dt.int32
+U32 = mybir.dt.uint32
+U16 = mybir.dt.uint16
+U8 = mybir.dt.uint8
+E4M3 = mybir.dt.float8_e4m3fn_x4
+E5M2 = mybir.dt.float8_e5m2_x4
+E2M1 = mybir.dt.float4_e2m1fn_x4
+ALU = mybir.AluOpType
+ACT = mybir.ActivationFunctionType
+
+P = 128
+PACK = 4
+JT = J // P
+LIST_COLS = P // 16
+
+
+def tile_list_rows_picked_peak_floored_pl_kernel(
+    tc, xt_words, xt_scales, w_words, w_scales, us, wb_words, wb_scales, tz, rw, offs, offs2, out_0, out_1, out_2
+):
+    nc = tc.nc
+    with ExitStack() as ctx:
+        sb = ctx.enter_context(tc.tile_pool(name="sb", bufs=1))
+        ps = ctx.enter_context(tc.psum_pool(name="ps", bufs=1))
+
+        def load_scales(tile, dram, queues):
+            for q in range(4):
+                queues[q].dma_start(
+                    out=tile[32 * q : 32 * q + 4, :].bitcast(I32), in_=dram[0, 4 * q : 4 * q + 4, :].bitcast(I32)
+                )
+
+        offs_sb = sb.tile([P, J // 16], U16, name="offs_sb")
+        offs2_sb = sb.tile([P, J // 16], U16, name="offs2_sb")
+        xw = sb.tile([P, T], U16, name="xw", align_bytes=64)
+        xs = sb.tile([P, T], U8, name="xs", align_bytes=64)
+        ww = sb.tile([P, R], U32, name="ww", align_bytes=64)
+        ws = sb.tile([P, R], U8, name="ws", align_bytes=64)
+        bw = sb.tile([P, N], U32, name="bw", align_bytes=64)
+        bs = sb.tile([P, N], U8, name="bs", align_bytes=64)
+        us_col = sb.tile([P, PACK], F32, name="us_col")
+        rw_col = sb.tile([P, 2], F32, name="rw_col")
+        tz_sb = [sb.tile([P, 2, Z], F32, name="tz_sb%d" % h) for h in range(2)]
+        ident = sb.tile([P, P], F32, name="ident")
+
+        nc.vector.memset(xs[:].bitcast(I32), 0)
+        nc.vector.memset(bs[:].bitcast(I32), 0)
+
+        nc.sync.dma_start(offs_sb[:], offs)
+        nc.sync.dma_start(out=xw[:].bitcast(I32), in_=xt_words[0].bitcast(I32))
+        load_scales(xs, xt_scales, [nc.scalar] * 4)
+        nc.sync.dma_start(out=ww[:].bitcast(I32), in_=w_words[0].rearrange("p n t -> p (n t)").bitcast(I32))
+        load_scales(ws, w_scales, [nc.gpsimd, nc.sync, nc.sync, nc.sync])
+        nc.gpsimd.dma_start(out=us_col[:], in_=us.rearrange("o (p t) -> (o p) t", t=PACK))
+        make_identity(nc, ident[:])
+        nc.sync.dma_start(offs2_sb[:], offs2)
+        tz_rows = tz.rearrange("(p t) z -> p t z", t=PACK)
+        for h in range(2):
+            nc.sync.dma_start(out=tz_sb[h][:], in_=tz_rows[:, 2 * h : 2 * h + 2, :])
+        nc.sync.dma_start(out=bw[:].bitcast(I32), in_=wb_words[0].rearrange("p n t -> p (n t)").bitcast(I32))
+        load_scales(bs, wb_scales, [nc.sync] * 4)
+        nc.gpsimd.dma_start(out=rw_col[:], in_=rw.rearrange("o (p e) -> (o p) e", e=2))
+
+        a_ps = []
+        for jt in range(JT):
+            lst = offs_sb[:, jt * LIST_COLS : (jt + 1) * LIST_COLS]
+            gw = sb.tile([P, P], U16, name="gw%d" % jt, align_bytes=64)
+            gs = sb.tile([P, P], U8, name="gs%d" % jt, align_bytes=64)
+            nc.vector.tensor_copy(gw[:], xw[:].indirect(lst))
+            nc.vector.tensor_copy(gs[:], xs[:].indirect(lst))
+            acc = ps.tile([P, R], F32, name="a_ps%d" % jt)
+            nc.tensor.matmul_mx(
+                out=acc[:], lhsT=gw[:].bitcast(E2M1), lhsT_scale=gs[:], rhs=ww[:].bitcast(E5M2), rhs_scale=ws[:],
+                start=True, stop=True,
+            )
+            a_ps.append(acc)
+
+        us_ps = ps.tile([P, 2, P, 2], F32, name="us_ps")
+        for t in range(PACK):
+            nc.tensor.transpose(us_ps[:, t // 2, :, t % 2], us_col[:, t : t + 1].to_broadcast([P, P]), ident[:])
+        rw_ps = ps.tile([P, P, 2], F32, name="rw_ps")
+        for e in range(2):
+            nc.tensor.transpose(rw_ps[:, :, e], rw_col[:, e : e + 1].to_broadcast([P, P]), ident[:])
+
+        tzg = sb.tile([P, PACK, J], F32, name="tzg")
+        for t in range(PACK):
+            nc.scalar.activation(tzg[:, t, :], tz_sb[t // 2][:, t % 2, :].indirect(offs2_sb[:]), ACT.Copy)
+
+        bwd = sb.tile([P, PACK, P], U32, name="bwd", align_bytes=64)
+        bsd = sb.tile([P, PACK, P], U8, name="bsd", align_bytes=64)
+        nc.gpsimd.tensor_copy(bwd[:], bw[:].rearrange("p (m t) -> p t m", t=PACK))
+        nc.gpsimd.tensor_copy(bsd[:], bs[:].rearrange("p (m t) -> p t m", t=PACK))
+
+        pos = [sb.tile([P, R], F32, name="pos%d" % jt) for jt in range(JT)]
+        peak = [sb.tile([P, 1], F32, name="peak%d" % jt) for jt in range(JT)]
+        den = [sb.tile([P, 1], F32, name="den%d" % jt) for jt in range(JT)]
+        inv = [sb.tile([P, 1], F32, name="inv%d" % jt) for jt in range(JT)]
+        hr = [sb.tile([P, R], BF16, name="hr%d" % jt, align_bytes=64) for jt in range(JT)]
+        for jt in range(JT):
+            nc.vector.tensor_scalar(
+                pos[jt][:].rearrange("j (u p e) -> j u p e", u=2, e=2),
+                a_ps[jt][:].rearrange("j (p u e) -> j u p e", u=2, e=2),
+                0.0, None, ALU.max, ALU.max, accum_out=peak[jt][:],
+            )
+        for jt in range(JT):
+            nc.vector.tensor_scalar(den[jt][:], peak[jt][:], 0.3, None, ALU.add)
+        for jt in range(JT):
+            nc.vector.reciprocal(inv[jt][:], den[jt][:])
+        hq = []
+        for jt in range(JT):
+            nc.vector.scalar_tensor_tensor(
+                hr[jt][:], pos[jt][:], inv[jt][:], us_ps[:].rearrange("j u p e -> j (u p e)"), ALU.mult, ALU.mult
+            )
+            pairs = hr[jt][:].bitcast(F32)
+            h_ps = ps.tile([P, 2, P], F32, name="h_ps%d" % jt)
+            for u in range(2):
+                nc.tensor.transpose(h_ps[:, u, :], pairs[:, u * P : (u + 1) * P], ident[:])
+            hid = sb.tile([P, P * PACK], BF16, name="hid%d" % jt, align_bytes=64)
+            nc.scalar.copy(hid[:].bitcast(F32).rearrange("p (j u) -> p j u", u=2), h_ps[:].rearrange("p u j -> p j u"))
+            hq.append(hid)
+
+        p_ps = []
+        for jt in range(JT):
+            hw = sb.tile([P, P], U32, name="hw%d" % jt, align_bytes=64)
+            hs = sb.tile([P, P], U8, name="hs%d" % jt, align_bytes=64)
+            nc.vector.quantize_mx(out=hw[:].bitcast(E5M2), scales=hs[:], in_=hq[jt][:])
+            acc = ps.tile([P, PACK, P], F32, name="p_ps%d" % jt)
+            for t in range(PACK):
+                nc.tensor.matmul_mx(
+                    out=acc[:, t, :], lhsT=bwd[:, t, :].bitcast(E4M3), lhsT_scale=bsd[:, t, :],
+                    rhs=hw[:].bitcast(E5M2), rhs_scale=hs[:], start=True, stop=True,
+                )
+            p_ps.append(acc)
+
+        y_rows = out_0.rearrange("(p t) j -> p t j", t=PACK)
+        words_out = out_1[0].rearrange("p j t -> p (j t)").bitcast(I32)
+        yw = sb.tile([P, J], U32, name="yw", align_bytes=64)
+        ys = sb.tile([P, J], U8, name="ys", align_bytes=64)
+        rw_row = rw_ps[:].rearrange("p q e -> p (q e)")
+        ybs = []
+        for jt in range(JT):
+            cols = slice(jt * P, (jt + 1) * P)
+            top = sb.tile([P, PACK, P], F32, name="top%d" % jt)
+            y = sb.tile([P, PACK, P], F32, name="y%d" % jt)
+            yb = sb.tile([P, P, PACK], BF16, name="yb%d" % jt, align_bytes=64)
+            nc.vector.tensor_tensor(top[:], p_ps[jt][:], tzg[:, :, cols], ALU.max)
+            nc.vector.tensor_tensor(y[:], top[:], rw_row[:, cols].unsqueeze(1).to_broadcast([P, PACK, P]), ALU.mult)
+            nc.sync.dma_start(out=y_rows[:, :, cols], in_=y[:])
+            nc.scalar.copy(yb[:], y[:].rearrange("p t j -> p j t"))
+            ybs.append(yb)
+        for jt in range(JT):
+            cols = slice(jt * P, (jt + 1) * P)
+            nc.vector.quantize_mx(
+                out=yw[:, cols].bitcast(E4M3), scales=ys[:, cols], in_=ybs[jt][:].rearrange("p j t -> p (j t)")
+            )
+            nc.sync.dma_start(out=words_out[:, cols], in_=yw[:, cols].bitcast(I32))
+        for q in range(4):
+            queue = nc.sync if q % 2 == 0 else nc.scalar
+            queue.dma_start(
+                out=out_2[0, 4 * q : 4 * q + 4, :].bitcast(I32), in_=ys[32 * q : 32 * q + 4, :].bitcast(I32)
+            )

@@ -32,11 +32,17 @@ def tile_list_rows_picked_peak_floored_pl_kernel(
         sb = ctx.enter_context(tc.tile_pool(name="sb", bufs=1))
         ps = ctx.enter_context(tc.psum_pool(name="ps", bufs=1))
 
-        def load_scales(tile, dram, queues):
-            for q in range(4):
-                queues[q].dma_start(
-                    out=tile[32 * q : 32 * q + 4, :].bitcast(I32), in_=dram[0, 4 * q : 4 * q + 4, :].bitcast(I32)
-                )
+        def load_scale_rows(queue, tile, dram, q):
+            queue.dma_start(
+                out=tile[32 * q : 32 * q + 4, :].bitcast(I32), in_=dram[0, 4 * q : 4 * q + 4, :].bitcast(I32)
+            )
+
+        def spread_scale_rows(queue, tile, dram, q):
+            rows = dram[0, 4 * q : 4 * q + 4, :].bitcast(I32)
+            queue.dma_start(
+                out=tile[32 * q : 32 * q + 32, :].bitcast(I32),
+                in_=rows.unsqueeze(0).to_broadcast([8, 4, rows.shape[1]]),
+            )
 
         offs_sb = sb.tile([P, J // 16], U16, name="offs_sb")
         offs2_sb = sb.tile([P, J // 16], U16, name="offs2_sb")
@@ -51,23 +57,30 @@ def tile_list_rows_picked_peak_floored_pl_kernel(
         tz_sb = [sb.tile([P, 2, Z], F32, name="tz_sb%d" % h) for h in range(2)]
         ident = sb.tile([P, P], F32, name="ident")
 
-        nc.vector.memset(xs[:].bitcast(I32), 0)
-        nc.vector.memset(bs[:].bitcast(I32), 0)
+        warm = sb.tile([P, 2], F32, name="warm")
+        nc.vector.memset(warm[:, 0:1], 0.0)
+        nc.vector.memset(ident[:], 0.0)
 
+        make_identity(nc, ident[:], nomemset=True)
         nc.sync.dma_start(offs_sb[:], offs)
         nc.sync.dma_start(out=xw[:].bitcast(I32), in_=xt_words[0].bitcast(I32))
-        load_scales(xs, xt_scales, [nc.scalar] * 4)
+        for q in range(3):
+            spread_scale_rows(nc.scalar, xs, xt_scales, q)
+        spread_scale_rows(nc.sync, xs, xt_scales, 3)
+        load_scale_rows(nc.scalar, ws, w_scales, 0)
         nc.sync.dma_start(out=ww[:].bitcast(I32), in_=w_words[0].rearrange("p n t -> p (n t)").bitcast(I32))
-        load_scales(ws, w_scales, [nc.gpsimd, nc.sync, nc.sync, nc.sync])
-        nc.gpsimd.dma_start(out=us_col[:], in_=us.rearrange("o (p t) -> (o p) t", t=PACK))
-        make_identity(nc, ident[:])
+        nc.scalar.activation(warm[:, 1:2], warm[:, 0:1], ACT.Copy)
+        for q in range(1, 4):
+            load_scale_rows(nc.sync, ws, w_scales, q)
         nc.sync.dma_start(offs2_sb[:], offs2)
         tz_rows = tz.rearrange("(p t) z -> p t z", t=PACK)
-        for h in range(2):
-            nc.sync.dma_start(out=tz_sb[h][:], in_=tz_rows[:, 2 * h : 2 * h + 2, :])
+        nc.sync.dma_start(out=tz_sb[0][:], in_=tz_rows[:, 0:2, :])
+        nc.sync.dma_start(out=us_col[:], in_=us.rearrange("o (p t) -> (o p) t", t=PACK))
+        nc.sync.dma_start(out=tz_sb[1][:], in_=tz_rows[:, 2:4, :])
         nc.sync.dma_start(out=bw[:].bitcast(I32), in_=wb_words[0].rearrange("p n t -> p (n t)").bitcast(I32))
-        load_scales(bs, wb_scales, [nc.sync] * 4)
-        nc.gpsimd.dma_start(out=rw_col[:], in_=rw.rearrange("o (p e) -> (o p) e", e=2))
+        for q in range(4):
+            spread_scale_rows(nc.sync, bs, wb_scales, q)
+        nc.sync.dma_start(out=rw_col[:], in_=rw.rearrange("o (p e) -> (o p) e", e=2))
 
         a_ps = []
         for jt in range(JT):
@@ -76,33 +89,27 @@ def tile_list_rows_picked_peak_floored_pl_kernel(
             gs = sb.tile([P, P], U8, name="gs%d" % jt, align_bytes=64)
             nc.vector.tensor_copy(gw[:], xw[:].indirect(lst))
             nc.vector.tensor_copy(gs[:], xs[:].indirect(lst))
-            acc = ps.tile([P, R], F32, name="a_ps%d" % jt)
+            acc = ps.tile([P, R], F32, name="a_ps%d" % jt, tag="acc%d" % jt)
             nc.tensor.matmul_mx(
                 out=acc[:], lhsT=gw[:].bitcast(E2M1), lhsT_scale=gs[:], rhs=ww[:].bitcast(E5M2), rhs_scale=ws[:],
                 start=True, stop=True,
             )
             a_ps.append(acc)
 
-        us_ps = ps.tile([P, 2, P, 2], F32, name="us_ps")
+
+        us_ps = ps.tile([P, 2, P, 2], F32, name="us_ps", tag="us_ps")
         for t in range(PACK):
             nc.tensor.transpose(us_ps[:, t // 2, :, t % 2], us_col[:, t : t + 1].to_broadcast([P, P]), ident[:])
-        rw_ps = ps.tile([P, P, 2], F32, name="rw_ps")
-        for e in range(2):
-            nc.tensor.transpose(rw_ps[:, :, e], rw_col[:, e : e + 1].to_broadcast([P, P]), ident[:])
 
         tzg = sb.tile([P, PACK, J], F32, name="tzg")
         for t in range(PACK):
             nc.scalar.activation(tzg[:, t, :], tz_sb[t // 2][:, t % 2, :].indirect(offs2_sb[:]), ACT.Copy)
 
-        bwd = sb.tile([P, PACK, P], U32, name="bwd", align_bytes=64)
-        bsd = sb.tile([P, PACK, P], U8, name="bsd", align_bytes=64)
-        nc.gpsimd.tensor_copy(bwd[:], bw[:].rearrange("p (m t) -> p t m", t=PACK))
-        nc.gpsimd.tensor_copy(bsd[:], bs[:].rearrange("p (m t) -> p t m", t=PACK))
 
-        pos = [sb.tile([P, R], F32, name="pos%d" % jt) for jt in range(JT)]
+        pos = [sb.tile([P, R], F32, name="pos%d" % jt, tag="pos%d" % jt, align_bytes=64) for jt in range(JT)]
         peak = [sb.tile([P, 1], F32, name="peak%d" % jt) for jt in range(JT)]
         den = [sb.tile([P, 1], F32, name="den%d" % jt) for jt in range(JT)]
-        inv = [sb.tile([P, 1], F32, name="inv%d" % jt) for jt in range(JT)]
+        inv = [sb.tile([P, 1], F32, name="inv%d" % jt, tag="inv%d" % jt, align_bytes=64) for jt in range(JT)]
         hr = [sb.tile([P, R], BF16, name="hr%d" % jt, align_bytes=64) for jt in range(JT)]
         for jt in range(JT):
             nc.vector.tensor_scalar(
@@ -127,41 +134,54 @@ def tile_list_rows_picked_peak_floored_pl_kernel(
             nc.scalar.copy(hid[:].bitcast(F32).rearrange("p (j u) -> p j u", u=2), h_ps[:].rearrange("p u j -> p j u"))
             hq.append(hid)
 
+        rw_ps = ps.tile([P, P, 2], F32, name="rw_ps", tag="us_ps")
+        for e in range(2):
+            nc.tensor.transpose(rw_ps[:, :, e], rw_col[:, e : e + 1].to_broadcast([P, P]), ident[:])
+        bwd = sb.tile([P, PACK, P], U32, name="bwd", tag="pos1", align_bytes=64)
+        bsd = sb.tile([P, PACK, P], U8, name="bsd", tag="inv1", align_bytes=64)
+        nc.vector.tensor_copy(bwd[:], bw[:].rearrange("p (m t) -> p t m", t=PACK))
+        nc.vector.tensor_copy(bsd[:], bs[:].rearrange("p (m t) -> p t m", t=PACK))
         p_ps = []
         for jt in range(JT):
             hw = sb.tile([P, P], U32, name="hw%d" % jt, align_bytes=64)
             hs = sb.tile([P, P], U8, name="hs%d" % jt, align_bytes=64)
             nc.vector.quantize_mx(out=hw[:].bitcast(E5M2), scales=hs[:], in_=hq[jt][:])
-            acc = ps.tile([P, PACK, P], F32, name="p_ps%d" % jt)
+            banks = [ps.tile([P, 2, P], F32, name="p_ps%d_%d" % (jt, u), tag=("acc%d" % u if jt == 1 else "p%d" % u)) for u in range(2)]
             for t in range(PACK):
                 nc.tensor.matmul_mx(
-                    out=acc[:, t, :], lhsT=bwd[:, t, :].bitcast(E4M3), lhsT_scale=bsd[:, t, :],
+                    out=banks[t // 2][:, t % 2, :], lhsT=bwd[:, t, :].bitcast(E4M3), lhsT_scale=bsd[:, t, :],
                     rhs=hw[:].bitcast(E5M2), rhs_scale=hs[:], start=True, stop=True,
                 )
-            p_ps.append(acc)
+            p_ps.append(banks)
 
         y_rows = out_0.rearrange("(p t) j -> p t j", t=PACK)
         words_out = out_1[0].rearrange("p j t -> p (j t)").bitcast(I32)
         yw = sb.tile([P, J], U32, name="yw", align_bytes=64)
         ys = sb.tile([P, J], U8, name="ys", align_bytes=64)
         rw_row = rw_ps[:].rearrange("p q e -> p (q e)")
-        ybs = []
+        pieces = []
         for jt in range(JT):
             cols = slice(jt * P, (jt + 1) * P)
             top = sb.tile([P, PACK, P], F32, name="top%d" % jt)
             y = sb.tile([P, PACK, P], F32, name="y%d" % jt)
-            yb = sb.tile([P, P, PACK], BF16, name="yb%d" % jt, align_bytes=64)
-            nc.vector.tensor_tensor(top[:], p_ps[jt][:], tzg[:, :, cols], ALU.max)
-            nc.vector.tensor_tensor(y[:], top[:], rw_row[:, cols].unsqueeze(1).to_broadcast([P, PACK, P]), ALU.mult)
+            for u in range(2):
+                ts = slice(2 * u, 2 * u + 2)
+                nc.vector.tensor_tensor(top[:, ts, :], p_ps[jt][u][:], tzg[:, ts, cols], ALU.max)
+            width = P if jt < JT - 1 else P // 2
+            for lo in range(0, P, width):
+                part = slice(lo, lo + width)
+                whole = slice(jt * P + lo, jt * P + lo + width)
+                yb = sb.tile([P, width, PACK], BF16, name="yb%d_%d" % (jt, lo), align_bytes=64)
+                weight = rw_row[:, whole].unsqueeze(1).to_broadcast([P, PACK, width])
+                nc.vector.tensor_tensor(y[:, :, part], top[:, :, part], weight, ALU.mult)
+                nc.scalar.copy(yb[:], y[:, :, part].rearrange("p t j -> p j t"))
+                pieces.append((whole, yb))
             nc.sync.dma_start(out=y_rows[:, :, cols], in_=y[:])
-            nc.scalar.copy(yb[:], y[:].rearrange("p t j -> p j t"))
-            ybs.append(yb)
-        for jt in range(JT):
-            cols = slice(jt * P, (jt + 1) * P)
+        for cols, yb in pieces:
             nc.vector.quantize_mx(
-                out=yw[:, cols].bitcast(E4M3), scales=ys[:, cols], in_=ybs[jt][:].rearrange("p j t -> p (j t)")
+                out=yw[:, cols].bitcast(E4M3), scales=ys[:, cols], in_=yb[:].rearrange("p j t -> p (j t)")
             )
-            nc.sync.dma_start(out=words_out[:, cols], in_=yw[:, cols].bitcast(I32))
+        nc.sync.dma_start(out=words_out, in_=yw[:].bitcast(I32))
         for q in range(4):
             queue = nc.sync if q % 2 == 0 else nc.scalar
             queue.dma_start(

@@ -69,17 +69,18 @@ def tile_list_rows_picked_peak_floored_pl_kernel(
         spread_scale_rows(nc.sync, xs, xt_scales, 3)
         load_scale_rows(nc.scalar, ws, w_scales, 0)
         nc.sync.dma_start(out=ww[:].bitcast(I32), in_=w_words[0].rearrange("p n t -> p (n t)").bitcast(I32))
-        nc.scalar.activation(warm[:, 1:2], warm[:, 0:1], ACT.Copy)
-        for q in range(1, 4):
-            load_scale_rows(nc.sync, ws, w_scales, q)
-        nc.sync.dma_start(offs2_sb[:], offs2)
-        tz_rows = tz.rearrange("(p t) z -> p t z", t=PACK)
-        nc.sync.dma_start(out=tz_sb[0][:], in_=tz_rows[:, 0:2, :])
-        nc.sync.dma_start(out=us_col[:], in_=us.rearrange("o (p t) -> (o p) t", t=PACK))
-        nc.sync.dma_start(out=tz_sb[1][:], in_=tz_rows[:, 2:4, :])
+        load_scale_rows(nc.scalar, ws, w_scales, 1)
+        load_scale_rows(nc.sync, ws, w_scales, 2)
+        load_scale_rows(nc.sync, ws, w_scales, 3)
         nc.sync.dma_start(out=bw[:].bitcast(I32), in_=wb_words[0].rearrange("p n t -> p (n t)").bitcast(I32))
         for q in range(4):
-            spread_scale_rows(nc.sync, bs, wb_scales, q)
+            spread_scale_rows(nc.scalar if q < 2 else nc.sync, bs, wb_scales, q)
+        nc.scalar.activation(warm[:, 1:2], warm[:, 0:1], ACT.Copy)
+        nc.sync.dma_start(out=us_col[:], in_=us.rearrange("o (p t) -> (o p) t", t=PACK))
+        nc.sync.dma_start(offs2_sb[:], offs2)
+        tz_rows = tz.rearrange("(p t) z -> p t z", t=PACK)
+        for h in range(2):
+            nc.sync.dma_start(out=tz_sb[h][:], in_=tz_rows[:, 2 * h : 2 * h + 2, :])
         nc.sync.dma_start(out=rw_col[:], in_=rw.rearrange("o (p e) -> (o p) e", e=2))
 
         a_ps = []
@@ -96,6 +97,15 @@ def tile_list_rows_picked_peak_floored_pl_kernel(
             )
             a_ps.append(acc)
 
+
+        bwd = sb.tile([P, PACK, P], U32, name="bwd", align_bytes=64)
+        bsd = sb.tile([P, PACK, P], U8, name="bsd", align_bytes=64)
+        nc.vector.tensor_copy(
+            bwd[:].rearrange("p t (b i) -> p b t i", i=4), bw[:].rearrange("p (b i t) -> p b t i", i=4, t=PACK)
+        )
+        nc.vector.tensor_copy(
+            bsd[:].rearrange("p t (b i) -> p b t i", i=16), bs[:].rearrange("p (b i t) -> p b t i", i=16, t=PACK)
+        )
 
         us_ps = ps.tile([P, 2, P, 2], F32, name="us_ps", tag="us_ps")
         for t in range(PACK):
@@ -131,16 +141,13 @@ def tile_list_rows_picked_peak_floored_pl_kernel(
             for u in range(2):
                 nc.tensor.transpose(h_ps[:, u, :], pairs[:, u * P : (u + 1) * P], ident[:])
             hid = sb.tile([P, P * PACK], BF16, name="hid%d" % jt, align_bytes=64)
-            nc.scalar.copy(hid[:].bitcast(F32).rearrange("p (j u) -> p j u", u=2), h_ps[:].rearrange("p u j -> p j u"))
+            move = nc.vector.tensor_copy if jt == 0 else nc.scalar.copy
+            move(hid[:].bitcast(F32).rearrange("p (j u) -> p j u", u=2), h_ps[:].rearrange("p u j -> p j u"))
             hq.append(hid)
 
         rw_ps = ps.tile([P, P, 2], F32, name="rw_ps", tag="us_ps")
         for e in range(2):
             nc.tensor.transpose(rw_ps[:, :, e], rw_col[:, e : e + 1].to_broadcast([P, P]), ident[:])
-        bwd = sb.tile([P, PACK, P], U32, name="bwd", tag="pos1", align_bytes=64)
-        bsd = sb.tile([P, PACK, P], U8, name="bsd", tag="inv1", align_bytes=64)
-        nc.vector.tensor_copy(bwd[:], bw[:].rearrange("p (m t) -> p t m", t=PACK))
-        nc.vector.tensor_copy(bsd[:], bs[:].rearrange("p (m t) -> p t m", t=PACK))
         p_ps = []
         for jt in range(JT):
             hw = sb.tile([P, P], U32, name="hw%d" % jt, align_bytes=64)
@@ -174,14 +181,19 @@ def tile_list_rows_picked_peak_floored_pl_kernel(
                 yb = sb.tile([P, width, PACK], BF16, name="yb%d_%d" % (jt, lo), align_bytes=64)
                 weight = rw_row[:, whole].unsqueeze(1).to_broadcast([P, PACK, width])
                 nc.vector.tensor_tensor(y[:, :, part], top[:, :, part], weight, ALU.mult)
-                nc.scalar.copy(yb[:], y[:, :, part].rearrange("p t j -> p j t"))
+                if whole.stop < J:
+                    nc.scalar.copy(yb[:], y[:, :, part].rearrange("p t j -> p j t"))
+                else:
+                    nc.vector.tensor_copy(yb[:], y[:, :, part].rearrange("p t j -> p j t"))
                 pieces.append((whole, yb))
             nc.sync.dma_start(out=y_rows[:, :, cols], in_=y[:])
         for cols, yb in pieces:
             nc.vector.quantize_mx(
                 out=yw[:, cols].bitcast(E4M3), scales=ys[:, cols], in_=yb[:].rearrange("p j t -> p (j t)")
             )
-        nc.sync.dma_start(out=words_out, in_=yw[:].bitcast(I32))
+            if cols.stop == P:
+                nc.sync.dma_start(out=words_out[:, 0:P], in_=yw[:, 0:P].bitcast(I32))
+        nc.scalar.dma_start(out=words_out[:, P:J], in_=yw[:, P:J].bitcast(I32))
         for q in range(4):
             queue = nc.sync if q % 2 == 0 else nc.scalar
             queue.dma_start(

@@ -61,7 +61,6 @@ def tile_list_rows_picked_peak_floored_pl_kernel(
         nc.vector.memset(warm[:, 0:1], 0.0)
         nc.vector.memset(ident[:], 0.0)
 
-        make_identity(nc, ident[:], nomemset=True)
         nc.sync.dma_start(offs_sb[:], offs)
         nc.sync.dma_start(out=xw[:].bitcast(I32), in_=xt_words[0].bitcast(I32))
         for q in range(3):
@@ -73,14 +72,18 @@ def tile_list_rows_picked_peak_floored_pl_kernel(
         load_scale_rows(nc.sync, ws, w_scales, 2)
         load_scale_rows(nc.sync, ws, w_scales, 3)
         nc.sync.dma_start(out=bw[:].bitcast(I32), in_=wb_words[0].rearrange("p n t -> p (n t)").bitcast(I32))
-        for q in range(4):
-            spread_scale_rows(nc.scalar if q < 2 else nc.sync, bs, wb_scales, q)
+        nc.gpsimd.memset(bs[0:64, :].bitcast(I32), 0)
+        for q in range(2):
+            load_scale_rows(nc.gpsimd, bs, wb_scales, q)
+        make_identity(nc, ident[:], nomemset=True)
+        spread_scale_rows(nc.scalar, bs, wb_scales, 2)
+        spread_scale_rows(nc.sync, bs, wb_scales, 3)
         nc.scalar.activation(warm[:, 1:2], warm[:, 0:1], ACT.Copy)
         nc.sync.dma_start(out=us_col[:], in_=us.rearrange("o (p t) -> (o p) t", t=PACK))
-        nc.sync.dma_start(offs2_sb[:], offs2)
         tz_rows = tz.rearrange("(p t) z -> p t z", t=PACK)
-        for h in range(2):
-            nc.sync.dma_start(out=tz_sb[h][:], in_=tz_rows[:, 2 * h : 2 * h + 2, :])
+        nc.sync.dma_start(out=tz_sb[0][:], in_=tz_rows[:, 0:2, :])
+        nc.sync.dma_start(offs2_sb[:], offs2)
+        nc.sync.dma_start(out=tz_sb[1][:], in_=tz_rows[:, 2:4, :])
         nc.sync.dma_start(out=rw_col[:], in_=rw.rearrange("o (p e) -> (o p) e", e=2))
 
         a_ps = []
@@ -112,8 +115,13 @@ def tile_list_rows_picked_peak_floored_pl_kernel(
             nc.tensor.transpose(us_ps[:, t // 2, :, t % 2], us_col[:, t : t + 1].to_broadcast([P, P]), ident[:])
 
         tzg = sb.tile([P, PACK, J], F32, name="tzg")
-        for t in range(PACK):
-            nc.scalar.activation(tzg[:, t, :], tz_sb[t // 2][:, t % 2, :].indirect(offs2_sb[:]), ACT.Copy)
+        for h in range(2):
+            for jt in range(JT):
+                lst = offs2_sb[:, jt * LIST_COLS : (jt + 1) * LIST_COLS]
+                for e in range(2):
+                    nc.scalar.activation(
+                        tzg[:, 2 * h + e, jt * P : (jt + 1) * P], tz_sb[h][:, e, :].indirect(lst), ACT.Copy
+                    )
 
 
         pos = [sb.tile([P, R], F32, name="pos%d" % jt, tag="pos%d" % jt, align_bytes=64) for jt in range(JT)]

from contextlib import ExitStack

import concourse.mybir as mybir
from concourse.masks import make_identity

K, T, J, R, N, Z = 512, 512, 256, 512, 512, 512
FLOPS = 2 * J * K * R + 2 * J * R * N

F32 = mybir.dt.float32
BF16 = mybir.dt.bfloat16
I32 = mybir.dt.int32
U32 = mybir.dt.uint32
U16 = mybir.dt.uint16
U8 = mybir.dt.uint8
E4M3 = mybir.dt.float8_e4m3fn_x4
E5M2 = mybir.dt.float8_e5m2_x4
E2M1 = mybir.dt.float4_e2m1fn_x4
ALU = mybir.AluOpType
ACT = mybir.ActivationFunctionType

P = 128
PACK = 4
JT = J // P
LIST_COLS = P // 16


def tile_list_rows_picked_peak_floored_pl_kernel(
    tc, xt_words, xt_scales, w_words, w_scales, us, wb_words, wb_scales, tz, rw, offs, offs2, out_0, out_1, out_2
):
    nc = tc.nc
    with ExitStack() as ctx:
        sb = ctx.enter_context(tc.tile_pool(name="sb", bufs=1))
        ps = ctx.enter_context(tc.psum_pool(name="ps", bufs=1))

        def load_scale_rows(queue, tile, dram, q):
            queue.dma_start(
                out=tile[32 * q : 32 * q + 4, :].bitcast(I32), in_=dram[0, 4 * q : 4 * q + 4, :].bitcast(I32)
            )

        def spread_scale_rows(queue, tile, dram, q):
            rows = dram[0, 4 * q : 4 * q + 4, :].bitcast(I32)
            queue.dma_start(
                out=tile[32 * q : 32 * q + 32, :].bitcast(I32),
                in_=rows.unsqueeze(0).to_broadcast([8, 4, rows.shape[1]]),
            )

        offs_sb = sb.tile([P, J // 16], U16, name="offs_sb")
        offs2_sb = sb.tile([P, J // 16], U16, name="offs2_sb")
        xw = sb.tile([P, T], U16, name="xw", align_bytes=64)
        xs = sb.tile([P, T], U8, name="xs", align_bytes=64)
        ww = sb.tile([P, R], U32, name="ww", align_bytes=64)
        ws = sb.tile([P, R], U8, name="ws", align_bytes=64)
        bw = sb.tile([P, N], U32, name="bw", align_bytes=64)
        bs = sb.tile([P, N], U8, name="bs", align_bytes=64)
        us_col = sb.tile([P, PACK], F32, name="us_col")
        rw_col = sb.tile([P, 2], F32, name="rw_col")
        tz_sb = [sb.tile([P, 2, Z], F32, name="tz_sb%d" % h) for h in range(2)]
        ident = sb.tile([P, P], F32, name="ident")

        warm = sb.tile([P, 2], F32, name="warm")
        nc.vector.memset(warm[:, 0:1], 0.0)
        nc.vector.memset(ident[:], 0.0)

        nc.sync.dma_start(offs_sb[:], offs)
        nc.sync.dma_start(out=xw[:].bitcast(I32), in_=xt_words[0].bitcast(I32))
        for q in range(3):
            spread_scale_rows(nc.scalar, xs, xt_scales, q)
        spread_scale_rows(nc.sync, xs, xt_scales, 3)
        load_scale_rows(nc.scalar, ws, w_scales, 0)
        nc.sync.dma_start(out=ww[:].bitcast(I32), in_=w_words[0].rearrange("p n t -> p (n t)").bitcast(I32))
        load_scale_rows(nc.scalar, ws, w_scales, 1)
        load_scale_rows(nc.sync, ws, w_scales, 2)
        load_scale_rows(nc.sync, ws, w_scales, 3)
        nc.sync.dma_start(out=bw[:].bitcast(I32), in_=wb_words[0].rearrange("p n t -> p (n t)").bitcast(I32))
        nc.gpsimd.memset(bs[0:64, :].bitcast(I32), 0)
        for q in range(2):
            load_scale_rows(nc.gpsimd, bs, wb_scales, q)
        make_identity(nc, ident[:], nomemset=True)
        spread_scale_rows(nc.scalar, bs, wb_scales, 2)
        spread_scale_rows(nc.sync, bs, wb_scales, 3)
        nc.scalar.activation(warm[:, 1:2], warm[:, 0:1], ACT.Copy)
        nc.sync.dma_start(out=us_col[:], in_=us.rearrange("o (p t) -> (o p) t", t=PACK))
        tz_rows = tz.rearrange("(p t) z -> p t z", t=PACK)
        nc.sync.dma_start(out=tz_sb[0][:], in_=tz_rows[:, 0:2, :])
        nc.sync.dma_start(offs2_sb[:], offs2)
        nc.sync.dma_start(out=tz_sb[1][:], in_=tz_rows[:, 2:4, :])
        nc.sync.dma_start(out=rw_col[:], in_=rw.rearrange("o (p e) -> (o p) e", e=2))

        a_ps = []
        for jt in range(JT):
            lst = offs_sb[:, jt * LIST_COLS : (jt + 1) * LIST_COLS]
            gw = sb.tile([P, P], U16, name="gw%d" % jt, align_bytes=64)
            gs = sb.tile([P, P], U8, name="gs%d" % jt, align_bytes=64)
            nc.vector.tensor_copy(gw[:], xw[:].indirect(lst))
            nc.vector.tensor_copy(gs[:], xs[:].indirect(lst))
            acc = ps.tile([P, R], F32, name="a_ps%d" % jt, tag="acc%d" % jt)
            nc.tensor.matmul_mx(
                out=acc[:], lhsT=gw[:].bitcast(E2M1), lhsT_scale=gs[:], rhs=ww[:].bitcast(E5M2), rhs_scale=ws[:],
                start=True, stop=True,
            )
            a_ps.append(acc)


        bwd = sb.tile([P, PACK, P], U32, name="bwd", align_bytes=64)
        bsd = sb.tile([P, PACK, P], U8, name="bsd", align_bytes=64)
        nc.vector.tensor_copy(
            bwd[:].rearrange("p t (b i) -> p b t i", i=4), bw[:].rearrange("p (b i t) -> p b t i", i=4, t=PACK)
        )
        nc.vector.tensor_copy(
            bsd[:].rearrange("p t (b i) -> p b t i", i=16), bs[:].rearrange("p (b i t) -> p b t i", i=16, t=PACK)
        )

        us_ps = ps.tile([P, 2, P, 2], F32, name="us_ps", tag="us_ps")
        for t in range(PACK):
            nc.tensor.transpose(us_ps[:, t // 2, :, t % 2], us_col[:, t : t + 1].to_broadcast([P, P]), ident[:])

        tzg = sb.tile([P, PACK, J], F32, name="tzg")
        for h in range(2):
            for jt in range(JT):
                lst = offs2_sb[:, jt * LIST_COLS : (jt + 1) * LIST_COLS]
                for e in range(2):
                    nc.scalar.activation(
                        tzg[:, 2 * h + e, jt * P : (jt + 1) * P], tz_sb[h][:, e, :].indirect(lst), ACT.Copy
                    )


        pos = [sb.tile([P, R], F32, name="pos%d" % jt, tag="pos%d" % jt, align_bytes=64) for jt in range(JT)]
        peak = [sb.tile([P, 1], F32, name="peak%d" % jt) for jt in range(JT)]
        den = [sb.tile([P, 1], F32, name="den%d" % jt) for jt in range(JT)]
        inv = [sb.tile([P, 1], F32, name="inv%d" % jt, tag="inv%d" % jt, align_bytes=64) for jt in range(JT)]
        hr = [sb.tile([P, R], BF16, name="hr%d" % jt, align_bytes=64) for jt in range(JT)]
        for jt in range(JT):
            nc.vector.tensor_scalar(
                pos[jt][:].rearrange("j (u p e) -> j u p e", u=2, e=2),
                a_ps[jt][:].rearrange("j (p u e) -> j u p e", u=2, e=2),
                0.0, None, ALU.max, ALU.max, accum_out=peak[jt][:],
            )
        for jt in range(JT):
            nc.vector.tensor_scalar(den[jt][:], peak[jt][:], 0.3, None, ALU.add)
        for jt in range(JT):
            nc.vector.reciprocal(inv[jt][:], den[jt][:])
        hq = []
        for jt in range(JT):
            nc.vector.scalar_tensor_tensor(
                hr[jt][:], pos[jt][:], inv[jt][:], us_ps[:].rearrange("j u p e -> j (u p e)"), ALU.mult, ALU.mult
            )
            pairs = hr[jt][:].bitcast(F32)
            h_ps = ps.tile([P, 2, P], F32, name="h_ps%d" % jt)
            for u in range(2):
                nc.tensor.transpose(h_ps[:, u, :], pairs[:, u * P : (u + 1) * P], ident[:])
            hid = sb.tile([P, P * PACK], BF16, name="hid%d" % jt, align_bytes=64)
            move = nc.vector.tensor_copy if jt == 0 else nc.scalar.copy
            move(hid[:].bitcast(F32).rearrange("p (j u) -> p j u", u=2), h_ps[:].rearrange("p u j -> p j u"))
            hq.append(hid)

        rw_ps = ps.tile([P, P, 2], F32, name="rw_ps", tag="us_ps")
        for e in range(2):
            nc.tensor.transpose(rw_ps[:, :, e], rw_col[:, e : e + 1].to_broadcast([P, P]), ident[:])
        p_ps = []
        for jt in range(JT):
            hw = sb.tile([P, P], U32, name="hw%d" % jt, align_bytes=64)
            hs = sb.tile([P, P], U8, name="hs%d" % jt, align_bytes=64)
            nc.vector.quantize_mx(out=hw[:].bitcast(E5M2), scales=hs[:], in_=hq[jt][:])
            banks = [ps.tile([P, 2, P], F32, name="p_ps%d_%d" % (jt, u), tag=("acc%d" % u if jt == 1 else "p%d" % u)) for u in range(2)]
            for t in range(PACK):
                nc.tensor.matmul_mx(
                    out=banks[t // 2][:, t % 2, :], lhsT=bwd[:, t, :].bitcast(E4M3), lhsT_scale=bsd[:, t, :],
                    rhs=hw[:].bitcast(E5M2), rhs_scale=hs[:], start=True, stop=True,
                )
            p_ps.append(banks)

        y_rows = out_0.rearrange("(p t) j -> p t j", t=PACK)
        words_out = out_1[0].rearrange("p j t -> p (j t)").bitcast(I32)
        yw = sb.tile([P, J], U32, name="yw", align_bytes=64)
        ys = sb.tile([P, J], U8, name="ys", align_bytes=64)
        rw_row = rw_ps[:].rearrange("p q e -> p (q e)")
        pieces = []
        for jt in range(JT):
            cols = slice(jt * P, (jt + 1) * P)
            top = sb.tile([P, PACK, P], F32, name="top%d" % jt)
            y = sb.tile([P, PACK, P], F32, name="y%d" % jt)
            for u in range(2):
                ts = slice(2 * u, 2 * u + 2)
                nc.vector.tensor_tensor(top[:, ts, :], p_ps[jt][u][:], tzg[:, ts, cols], ALU.max)
            width = P if jt < JT - 1 else P // 2
            for lo in range(0, P, width):
                part = slice(lo, lo + width)
                whole = slice(jt * P + lo, jt * P + lo + width)
                yb = sb.tile([P, width, PACK], BF16, name="yb%d_%d" % (jt, lo), align_bytes=64)
                weight = rw_row[:, whole].unsqueeze(1).to_broadcast([P, PACK, width])
                nc.vector.tensor_tensor(y[:, :, part], top[:, :, part], weight, ALU.mult)
                if whole.stop < J:
                    nc.scalar.copy(yb[:], y[:, :, part].rearrange("p t j -> p j t"))
                else:
                    nc.vector.tensor_copy(yb[:], y[:, :, part].rearrange("p t j -> p j t"))
                pieces.append((whole, yb))
            nc.sync.dma_start(out=y_rows[:, :, cols], in_=y[:])
        for cols, yb in pieces:
            nc.vector.quantize_mx(
                out=yw[:, cols].bitcast(E4M3), scales=ys[:, cols], in_=yb[:].rearrange("p j t -> p (j t)")
            )
            if cols.stop == P:
                nc.sync.dma_start(out=words_out[:, 0:P], in_=yw[:, 0:P].bitcast(I32))
        nc.scalar.dma_start(out=words_out[:, P:J], in_=yw[:, P:J].bitcast(I32))
        for q in range(4):
            queue = nc.sync if q % 2 == 0 else nc.scalar
            queue.dma_start(
                out=out_2[0, 4 * q : 4 * q + 4, :].bitcast(I32), in_=ys[32 * q : 32 * q + 4, :].bitcast(I32)
            )
